import numpy as np, ml_dtypes
CORES = [10,34,74,98]
N = 4
BF = ml_dtypes.bfloat16
def gentries(a):
    return np.ascontiguousarray(a.reshape(8, 16, -1).transpose(0, 2, 1)).reshape(8, -1)
def gtable(e):
    e = np.asarray(e); return np.ascontiguousarray(e.reshape(8, -1, 16).transpose(0, 2, 1)).reshape(128, -1).astype(np.int32)
def f(rng, *shape):
    return (rng.standard_normal(shape, dtype=np.float32) * np.exp2(rng.integers(-2, 3, shape[:-1] + (1,)))).astype(BF)
def wide(rng, *shape):
    v = f(rng, *shape).astype(np.float32); k = shape[:-2] + (1, shape[-1])
    return (v * np.exp2(rng.integers(-6, 7, k)) * (rng.random(k) > 0.0625)).astype(BF)
M, S, D, Q = 2048, 64, 8, 4
P = N // Q
def forest(rng, L, aside, bushy, zero=False):
    free = S + rng.permutation(M - S); n = S * (D - 1)
    chain = np.concatenate([np.arange(S)[:, None], free[:n].reshape(S, D - 1)], 1)
    p = np.arange(M); dep = np.full(M, -1); dep[chain] = np.arange(D); p[chain[:, 1:]] = chain[:, :-1]; rest = free[n:]
    if bushy:
        h = len(rest) // 2; p[rest[:h]] = rng.integers(0, S); p[rest[h:]] = chain[rng.integers(0, S), D - 2]
    else:
        lev = rng.integers(1, D, len(rest))
        for d in range(1, D):
            v = rest[lev == d]; p[v] = rng.choice(np.flatnonzero(dep == d - 1), len(v)); dep[v] = d
    kids = S + rng.permutation(M - S); o = kids[np.argsort(p[kids], kind="stable")]; q = p[o]
    sib = np.zeros(M, np.int64); sib[o] = np.arange(M - S) - np.searchsorted(q, q); c = np.bincount(q, minlength=M)
    base = rng.integers(0, 4096, M); step = 2 * rng.integers(0, 2048, M) + 1
    if zero: base[0] = 0
    x = np.where((c > 0) & (rng.random(M) < 0.7), (rng.random(M) * c).astype(np.int64), c + (rng.random(M) * (4096 - c)).astype(np.int64))
    x[chain[:, :-1]] = sib[chain[:, 1:]]
    e = np.flatnonzero(L < D - 1); b = chain[e, L[e]]; w = sib[chain[e, L[e] + 1]]; cb = c[b]
    other = (w + 1 + (rng.random(len(e)) * (cb - 1)).astype(np.int64)) % cb; none = cb + (rng.random(len(e)) * (4096 - cb)).astype(np.int64)
    x[b] = np.where((cb > 1) & (rng.random(len(e)) < aside), other, none)
    t = (base + step * x) % 4096
    k = np.zeros(M, np.int64); k[o] = (base[q] + step[q] * sib[o]) % 4096
    k[:S] = np.where(rng.random(S) < 0.5, t[:S], rng.integers(0, 4096, S))
    return p, k, t
def shards(rng, t, sc, tie):
    v = sc * 4096 + t; win = rng.integers(0, N, t.shape); u = rng.random((N,) + t.shape)
    o = np.where(rng.random(t.shape) < tie, sc * 4096 + (u * (t + 1)).astype(np.int64), (u * (v + 1)).astype(np.int64))
    o = np.where((np.arange(N)[:, None, None, None] == win) | (rng.random(o.shape) < 0.03125), v, np.minimum(o, v))
    return np.ascontiguousarray(o.transpose(0, 2, 1, 3)).reshape(N, 8, N * M).astype(np.int32)
def draw(rng, L, aside=0.5, bushy=False, tie=0.125, uneven=False, zero=False):
    a = [[forest(rng, L[q, g], aside, bushy, zero) for g in range(8)] for q in range(N)]
    p, k, t = [np.array([[a[q][g][i] for g in range(8)] for q in range(N)]) for i in range(3)]
    sc = rng.integers(0, 4096, t.shape)
    if uneven: sc = 4095 >> rng.integers(0, 13, t.shape)
    return {"par": np.stack([gtable(p[q]) for q in range(N)]), "tok": k.astype(np.int32), "best": shards(rng, t, sc, tie), "kv": f(rng, N, 128, Q * M)}
def setup_inputs(rng):
    return draw(rng, rng.integers(0, D, (N, 8, S)))
def setup_inputs_full(rng):
    return draw(rng, np.full((N, 8, S), D - 1))
def setup_inputs_cut(rng):
    return draw(rng, rng.choice(np.array([0, 1, D - 2]), (N, 8, S)), aside=0.0, zero=True)
def setup_inputs_ties(rng):
    return draw(rng, rng.integers(0, D, (N, 8, S)), tie=1.0)
def setup_inputs_bushy(rng):
    return draw(rng, rng.integers(0, D, (N, 8, S)), bushy=True)
def setup_inputs_spread(rng):
    d = draw(rng, rng.integers(0, D, (N, 8, S)), uneven=True); d["kv"] = wide(rng, N, 128, Q * M); return d
def check_inputs(d):
    bad = []; p = np.stack([gentries(a) for a in d["par"]]).astype(np.int64); k = d["tok"].astype(np.int64); b = d["best"]
    if not np.isfinite(d["kv"].astype(np.float32)).all(): bad.append("finite")
    if b.min() < 0 or b.max() >= 1 << 24: bad.append("best")
    if k.min() < 0 or k.max() > 4095: bad.append("tokens")
    if p.min() < 0 or p.max() >= M: return bad + ["parents"]
    if (p[:, :, :S] != np.arange(S)).any(): bad.append("roots")
    a = p
    for i in range(D - 2): a = np.take_along_axis(p, a, 2)
    if (a >= S).any(): bad.append("depth")
    w = np.sort((p * 4096 + k)[:, :, S:], axis=2)
    if (w[:, :, 1:] == w[:, :, :-1]).any(): bad.append("children")
    return bad
def reference(par, tok, best, kv):
    p = np.stack([gentries(a) for a in par]).astype(np.int64)
    t = np.max(best, axis=0).reshape(8, N, M).transpose(1, 0, 2) & 4095
    ok = (np.arange(M) < S) | (tok == np.take_along_axis(t, p, 2))
    a = np.broadcast_to(np.arange(M), p.shape); acc = np.ones(p.shape, bool); dep = np.zeros(p.shape, np.int64)
    for i in range(D):
        acc = acc & np.take_along_axis(ok, a, 2); dep = dep + (a >= S); a = np.take_along_axis(p, a, 2)
    y = np.zeros((N, 128, Q * S * D), BF)
    for r in range(N):
        out = y[r].reshape(8, 16, Q * S * D)
        for i in range(Q):
            q = P * i + r % P; k = kv[r][:, i * M:(i + 1) * M].reshape(8, 16, M)
            g, j = np.nonzero(acc[q])
            out[g, :, (i * S + a[q, g, j]) * D + dep[q, g, j]] = k[g, :, j]
    return {"y": y}

@@ -1,0 +1,349 @@
+from concourse.bass import DstId, RemoteDMATransfer
+from concourse.mybir import AluOpType, ActivationFunctionType
+
+OP = AluOpType
+AF = ActivationFunctionType
+REAL = 2112
+WIN = REAL + 1984
+
+SCRATCH = {
+    "bd": ("dram", [3, 128, 128], "int32"),
+    "own": ("sbuf", [128, 128], "int32"),
+    "land": ("sbuf", [128, 384], "int32"),
+    "mx": ("sbuf", [128, 384], "int32"),
+    "tgt": ("sbuf", [128, 128], "int32"),
+    "parw": ("sbuf", [128, 128], "int32"),
+    "tokd": ("sbuf", [128, 128], "int32"),
+    "plo32": ("sbuf", [128, 128], "int32"),
+    "phi32": ("sbuf", [128, 128], "int32"),
+    "plo": ("sbuf", [128, 128], "uint16"),
+    "phi": ("sbuf", [128, 128], "float16"),
+    "tk": ("sbuf", [128, 128], "float16"),
+    "cidx": ("sbuf", [128, 1], "int32"),
+    "c15": ("sbuf", [128, 1], "int32"),
+    "c4": ("sbuf", [128, 1], "int32"),
+    "pcol": ("sbuf", [128, 1], "float32"),
+    "gcol": ("sbuf", [128, 1], "float32"),
+    "bcol": ("sbuf", [128, 1], "float32"),
+    "y0": ("sbuf", [128, 128], "bfloat16"),
+    "u": ("sbuf", [128, 128], "bfloat16"),
+    "gx": ("sbuf", [128, 128], "bfloat16"),
+    "z1": ("sbuf", [128, 128], "bfloat16"),
+    "z": ("sbuf", [128, 128], "bfloat16"),
+    "k16": ("sbuf", [128, 128], "float32"),
+    "dumm": ("sbuf", [128, 128], "float32"),
+    "pq0": ("sbuf", [128, 128], "int32"),
+    "pq1": ("sbuf", [128, 128], "float32"),
+    "parq": ("sbuf", [128, 128], "float32"),
+    "sel": ("sbuf", [128, 2048], "float16"),
+    "wrp": ("sbuf", [128, 2048], "bfloat16"),
+    "park": ("sbuf", [128, 2048], "float32"),
+    "key": ("sbuf", [128, 2048], "int32"),
+    "eq": ("sbuf", [128, 1984], "bfloat16"),
+    "o1": ("sbuf", [128, 128], "float32"),
+    "o2": ("sbuf", [128, 128], "float32"),
+    "off": ("sbuf", [128, 128], "uint16"),
+    "jv": ("sbuf", [128, 1984], "float32"),
+    "nv": ("sbuf", [128, WIN], "float32"),
+    "ns": ("sbuf", [128, WIN], "float32"),
+    "mask": ("sbuf", [128, 64], "float32"),
+    "rst": ("sbuf", [128, 128], "float32"),
+    "m": ("sbuf", [128, 128], "float32"),
+    "sc": ("sbuf", [128, 128], "float32"),
+    "lst": ("sbuf", [128, 28], "uint16"),
+    "ln": ("sbuf", [128, 112], "uint16"),
+    "kv_s": ("sbuf", [128, 8192], "bfloat16"),
+    "yb": ("sbuf", [128, 2048], "bfloat16"),
+    "psa": ("psum", [128, 2048], "float32"),
+    "psb": ("psum", [128, 2048], "float32"),
+}
+SEMAPHORES = ["snd1", "snd2a", "snd2b", "gl0", "gl1"] + ["arr%d" % o for o in (1, 2, 3)] + ["e%d" % i for i in range(140)]
+
+
+def rank_program(g, core, T, topo):
+    r = T.rank_of(core)
+    if r is None:
+        return
+    V, S, P, Y = g.vector, g.scalar, g.tensor, g.sync
+    N = len(T.cores)
+    count, waited = {}, set()
+
+    def ev():
+        name = "e%d" % len(count)
+        count[name] = 0
+        return name
+
+    def inc(ins, name, n=1):
+        ins.then_inc(T.sem[name], n)
+        count[name] = count[name] + n
+        return name
+
+    def wait(q, *names):
+        for name in names:
+            q.wait_ge(T.sem[name], count[name])
+            waited.add(name)
+
+    def one(ins, n=1):
+        return inc(ins, ev(), n)
+
+    dst = {o: T.cores[(r + o) % N] for o in (1, 2, 3)}
+    order = (1, 3, 2)
+
+    lb = {}
+
+    def part(q):
+        return T.best[:, q * 2048:(q + 1) * 2048]
+
+    lb[1] = one(Y.dma_start(T.bd[0], part((r + 1) % N)), 16)
+    l_par = one(S.dma_start(T.parw[:], T.par[:]), 16)
+    lb[3] = one(Y.dma_start(T.bd[2], part((r + 3) % N)), 16)
+    lb[2] = one(S.dma_start(T.bd[1], part((r + 2) % N)), 16)
+    l_tok = one(S.dma_start(T.tokd[:], T.tok[:]), 16)
+    l_own = one(Y.dma_start(T.own[:], part(r)), 16)
+
+    flag = dict(allow_small_or_imprecise_dtypes=True)
+    i_y0 = one(g.iota(T.y0[:], [[-16, 8], [0, 16]], 0, 1, **flag))
+    i_c = one(g.iota(T.cidx[:], [[0, 1]], 0, 1))
+    i_u = one(g.iota(T.u[:], [[0, 8], [1, 16]], 0, 0, **flag))
+    for o in order:
+        d = dst[o]
+        rid, pid, _ = topo.addr(d)
+        wait(g, lb[o])
+        g.remote_dma(T.land[:, (o - 1) * 128:o * 128], T.bd[o - 1], T.sem["arr%d" % o], T.sem.snd1, pid, rid, topo.mask(core, d))
+    n_snd1 = sum(len(topo.engines(core, dst[o])) for o in order)
+    i_gx = one(g.iota(T.gx[:], [[1, 8], [0, 16]], 0, 0, **flag))
+    i_k = one(g.iota(T.k16[:], [[16, 128]], 2048, 0, **flag))
+    i_jv = one(g.iota(T.jv[:], [[1, 1984]], 64, 0, **flag))
+
+    wait(S, i_y0)
+    e_fill = one(S.activation(T.nv[:, 0:128], T.y0[:], AF.Silu, scale=0.0))
+    n = 128
+    while n < REAL:
+        wait(S, e_fill)
+        w = min(n, REAL - n)
+        e_fill = one(S.activation(T.nv[:, n:n + w], T.nv[:, 0:w], AF.Copy))
+        n = n + w
+
+    wait(V, i_y0)
+    e_sel = ev()
+    for b in range(16):
+        inc(V.tensor_scalar(T.sel[:, b * 128:(b + 1) * 128], T.y0[:], float(b), None, OP.is_equal), e_sel)
+    wait(V, i_c)
+    a = ev()
+    inc(V.tensor_scalar(T.c15[:], T.cidx[:], 15, None, OP.bitwise_and), a)
+    inc(V.tensor_scalar(T.c4[:], T.cidx[:], 4, None, OP.arith_shift_right), a)
+    wait(V, a)
+    e_col = ev()
+    inc(V.tensor_copy(T.pcol[:], T.c15[:]), e_col)
+    inc(V.tensor_copy(T.gcol[:], T.c4[:]), e_col)
+    wait(V, e_col)
+    e_b = one(V.tensor_scalar(T.bcol[:], T.pcol[:], -4096.0, 2048.0, OP.mult, OP.add))
+    wait(V, l_par)
+    e_hi = one(V.tensor_scalar(T.phi32[:], T.parw[:], 1920, None, OP.bitwise_and))
+    e_lo = one(V.tensor_scalar(T.plo32[:], T.parw[:], 127, None, OP.bitwise_and))
+    wait(V, e_hi)
+    e_phi = one(V.tensor_scalar(T.phi[:], T.phi32[:], 32.0, None, OP.mult))
+    wait(V, l_tok)
+    e_tk = one(V.tensor_scalar(T.tk[:], T.tokd[:], -2048.0, None, OP.add))
+    wait(V, e_lo)
+    e_plo = one(V.tensor_copy(T.plo[:], T.plo32[:]))
+    e_p0 = one(V.tensor_scalar(T.pq0[:], T.parw[:], 64.0, 2048.0, OP.is_lt, OP.mult))
+    wait(V, i_u)
+    e_mask = one(V.tensor_scalar(T.mask[:], T.u[:, 0:64], T.pcol[:], None, OP.is_equal))
+    e_rst = one(V.memset(T.rst[:], 1.0))
+    wait(V, e_p0)
+    e_p1 = one(V.tensor_tensor(T.pq1[:], T.pq0[:], T.parw[:], OP.add))
+    wait(V, i_gx)
+    e_z1 = one(V.tensor_scalar(T.z1[:], T.gx[:], T.gcol[:], 64.0, OP.not_equal, OP.mult))
+    wait(V, e_rst)
+    e_rst2 = one(V.memset(T.rst[:, 0:128:32], 0.0))
+    wait(V, e_z1)
+    e_z = one(V.tensor_tensor(T.z[:], T.z1[:], T.u[:], OP.add))
+    wait(V, i_k)
+    e_du = one(V.tensor_scalar(T.dumm[:], T.k16[:], T.pcol[:], None, OP.add))
+    wait(V, e_z)
+    e_wrp = ev()
+    for b in range(16):
+        inc(V.tensor_scalar(T.wrp[:, b * 128:(b + 1) * 128], T.z[:], float(b), None, OP.is_equal), e_wrp)
+    wait(V, e_du, e_p1)
+    e_pq = one(V.tensor_tensor(T.parq[:], T.pq1[:], T.dumm[:], OP.subtract))
+
+    wait(P, e_sel, e_phi)
+    pe_a = []
+    for q in range(4):
+        e = ev()
+        for b in range(4 * q, 4 * q + 4):
+            inc(P.matmul(T.psa[:, b * 128:(b + 1) * 128], T.sel[:, b * 128:(b + 1) * 128], T.phi[:], True, True), e)
+        pe_a.append(e)
+    wait(P, e_tk)
+    pe_b = []
+    for q in range(4):
+        e = ev()
+        for c in range(4 * q, 4 * q + 4):
+            inc(P.matmul(T.psb[:, c * 128:(c + 1) * 128], T.sel[:, c * 128:(c + 1) * 128], T.tk[:], True, True), e)
+        pe_b.append(e)
+
+    wait(S, e_b)
+    e_pk = ev()
+    for b in range(16):
+        if b % 4 == 0:
+            wait(S, pe_a[b // 4])
+        inc(S.activation(T.park[:, b:2048:16], T.psa[:, b * 128:(b + 1) * 128], AF.Identity, bias=T.bcol[:]), e_pk)
+
+    wait(V, e_pk)
+    e_key = ev()
+    for q in range(4):
+        wait(V, pe_b[q])
+        cs = slice(q * 512, (q + 1) * 512)
+        inc(V.tensor_tensor(T.key[:, cs], T.psb[:, cs], T.park[:, cs], OP.add), e_key)
+
+    wait(S, e_fill)
+    e_fill2 = one(S.activation(T.ns[:, 0:REAL], T.nv[:, 0:REAL], AF.Copy))
+
+    wait(V, l_own)
+    src = T.own[:]
+    for n, o in enumerate(order):
+        sender = T.cores[(r - o) % N]
+        V.wait_ge(T.sem["arr%d" % o], len(topo.engines(sender, core)))
+        e = one(V.tensor_tensor(T.mx[:, n * 128:(n + 1) * 128], src, T.land[:, (o - 1) * 128:o * 128], OP.max))
+        wait(V, e)
+        src = T.mx[:, n * 128:(n + 1) * 128]
+    e_tgt = one(V.tensor_scalar(T.tgt[:], src, 4095, None, OP.bitwise_and))
+    wait(V, e_tgt, e_key, e_plo)
+
+    def match(a, b):
+        return one(V.tensor_tensor(T.eq[:, (a - 4) * 16:(b - 4) * 16], T.tgt[:, 0:128].indirect(T.plo[:, a:b]),
+                                   T.key[:, a * 16:b * 16], OP.is_equal))
+
+    def gather_bits(a, b, bank):
+        e = ev()
+        for x in range(16):
+            inc(P.matmul(T.psa[:, 512 * bank:512 * bank + b - a], T.wrp[:, x * 128:(x + 1) * 128],
+                         T.eq[:, (a - 4) * 16 + x:(b - 4) * 16:16], x == 0, x == 15), e)
+        return e
+
+    def offsets(a, b, bank, e_ok):
+        cs = slice(a, b)
+        wait(V, e_ok)
+        e = one(V.tensor_tensor(T.o1[:, cs], T.psa[:, 512 * bank:512 * bank + b - a], T.parq[:, cs], OP.mult))
+        wait(V, e)
+        e = one(V.tensor_tensor(T.o2[:, cs], T.o1[:, cs], T.dumm[:, cs], OP.add))
+        wait(V, e)
+        return one(V.tensor_copy(T.off[:, cs], T.o2[:, cs]))
+
+    def scatter_v(a, b):
+        return one(V.tensor_copy(T.nv[:, 0:WIN].indirect(T.off[:, a:b]), T.jv[:, (a - 4) * 16:(b - 4) * 16]))
+
+    def scatter_s(a, b):
+        return one(S.activation(T.ns[:, 0:WIN].indirect(T.off[:, a:b]), T.jv[:, (a - 4) * 16:(b - 4) * 16], AF.Silu))
+
+    A0, A1, A2, B1, B2 = 4, 28, 66, 98, 128
+    m_a = match(A0, A2)
+    m_b1 = match(A2, 106)
+    wait(P, e_wrp, e_pk, m_a)
+    ok_a = gather_bits(A0, A2, 0)
+    wait(V, e_pq)
+    off_a = offsets(A0, A2, 0, ok_a)
+    m_b2 = match(106, B2)
+    wait(P, m_b1, m_b2)
+    ok_b = gather_bits(A2, B2, 1)
+    wait(S, e_fill2, i_jv, off_a)
+    s_a = scatter_s(A1, A2)
+    wait(V, e_fill2, i_jv, off_a)
+    v_a = scatter_v(A0, A1)
+    off_b = offsets(A2, B2, 1, ok_b)
+    wait(S, off_b, s_a)
+    s_b = scatter_s(B1, B2)
+    wait(V, off_b, v_a)
+    v_b = scatter_v(A2, B1)
+
+    Y.wait_ge(T.sem.snd1, n_snd1)
+    l_kv = one(Y.dma_start(T.kv_s[:], T.kv[:]), 16)
+
+    ys = [ev() for i in range(N)]
+    yv = [ev() for i in range(N)]
+    wait(S, l_kv)
+    e_root = ev()
+    for i in range(N):
+        inc(S.activation(T.yb[:, i * 512:(i + 1) * 512:8], T.kv_s[:, i * 2048:i * 2048 + 64], AF.Copy), e_root)
+    wait(S, e_root)
+    e_zero = one(S.activation(T.kv_s[:, 0:8192:2048], T.kv_s[:, 0:8192:2048], AF.Copy, scale=0.0))
+    wait(S, e_zero)
+
+    def step(d):
+        e = ev()
+        if d == 1:
+            inc(V.tensor_tensor(T.m[:, 0:128:2], T.nv[:, 2048:2112], T.mask[:], OP.mult), e)
+            inc(V.tensor_tensor(T.m[:, 1:128:2], T.ns[:, 2048:2112], T.mask[:], OP.mult), e)
+        else:
+            cs = slice(4 * (d - 2), 4 * (d - 1))
+            inc(V.tensor_tensor(T.m[:, 0:128:2], T.nv[:, 0:REAL].indirect(T.lst[:, cs]), T.mask[:], OP.mult), e)
+            inc(V.tensor_tensor(T.m[:, 1:128:2], T.ns[:, 0:REAL].indirect(T.lst[:, cs]), T.mask[:], OP.mult), e)
+        wait(V, e)
+        e = one(V.tensor_tensor_scan(T.sc[:], T.rst[:], T.m[:], 0.0, OP.mult, OP.add))
+        wait(V, e)
+        e = one(V.tensor_scalar(T.lst[:, 4 * (d - 1):4 * d], T.sc[:, 31:128:32], 0.25, None, OP.add))
+        wait(V, e)
+        return e
+
+    wait(V, v_b, s_b, e_mask, e_rst2)
+    e_l = {}
+    for d in range(1, 8):
+        e_l[d] = step(d)
+
+    mask = topo.mask(core, dst[1]) & topo.mask(core, dst[2]) & topo.mask(core, dst[3])
+    bits = bin(mask).count("1")
+    ids = []
+    for o in order:
+        rid, pid, _ = topo.addr(dst[o])
+        ids.append(DstId(rid=rid, pnc=pid))
+    for b, (d, c0, c1) in enumerate(((4, 0, 16), (7, 16, 28))):
+        wait(g, e_l[d])
+        g.remote_dma_fused([RemoteDMATransfer(dst_ids=ids, dma_engine_mask=mask, remote_sem=T.sem["gl%d" % b],
+                                              srcs=[T.lst[:, c0:c1]], dsts=[T.ln[:, r * 28 + c0:r * 28 + c1] for _ in ids])],
+                           local_sem=T.sem["snd2a" if b == 0 else "snd2b"])
+
+    def pick(q, i, d):
+        lists = T.lst[:, 4 * (d - 1):4 * d] if i == r else T.ln[:, i * 28 + 4 * (d - 1):i * 28 + 4 * d]
+        out = T.yb[:, i * 512 + d:(i + 1) * 512:8]
+        win = T.kv_s[:, i * 2048:(i + 1) * 2048].indirect(lists)
+        if q == 0:
+            inc(V.tensor_copy(out, win), yv[i])
+        else:
+            inc(S.activation(out, win, AF.Copy), ys[i])
+
+    def arrived(q, b):
+        q.wait_ge(T.sem["gl%d" % b], bits * (N - 1))
+
+    others = [i for i in range(N) if i != r]
+    wait(V, e_zero)
+    for d in range(1, 5):
+        wait(S, e_l[d])
+        pick(1, r, d)
+    for d in range(5, 8):
+        pick(0, r, d)
+    wait(Y, yv[r], ys[r], e_root)
+    stores = [one(Y.dma_start(T.y[:, r * 512:(r + 1) * 512], T.yb[:, r * 512:(r + 1) * 512]), 16)]
+    arrived(V, 0)
+    arrived(S, 0)
+    for i in others:
+        pick(0, i, 1)
+        pick(0, i, 2)
+        pick(1, i, 3)
+        pick(1, i, 4)
+    arrived(V, 1)
+    arrived(S, 1)
+    for n, i in enumerate(others):
+        pick(0, i, 5)
+        pick(n % 2, i, 6)
+        pick(1, i, 7)
+    for i in others:
+        wait(Y, yv[i], ys[i])
+        stores.append(one(Y.dma_start(T.y[:, i * 512:(i + 1) * 512], T.yb[:, i * 512:(i + 1) * 512]), 16))
+    for e in stores:
+        wait(Y, e)
+    g.wait_ge(T.sem.snd2a, bits)
+    g.wait_ge(T.sem.snd2b, bits)
+    for e in list(count):
+        if e not in waited and count[e]:
+            wait(g, e)

@@ -5,19 +5,24 @@ OP = AluOpType
 AF = ActivationFunctionType
 REAL = 2112
 WIN = REAL + 1984
+EARLY = 512
+BATCHES = (4, 32, 74, 128)
+S_PART = ((4, 32), (50, 74), (102, 128))
+HV = 4
+LISTS = ((4, 0, 16), (7, 16, 28))
 
 SCRATCH = {
     "bd": ("dram", [3, 128, 128], "int32"),
     "own": ("sbuf", [128, 128], "int32"),
     "land": ("sbuf", [128, 384], "int32"),
-    "mx": ("sbuf", [128, 384], "int32"),
+    "mx": ("sbuf", [128, 128], "int32"),
     "tgt": ("sbuf", [128, 128], "int32"),
     "parw": ("sbuf", [128, 128], "int32"),
     "tokd": ("sbuf", [128, 128], "int32"),
     "plo32": ("sbuf", [128, 128], "int32"),
     "phi32": ("sbuf", [128, 128], "int32"),
     "plo": ("sbuf", [128, 128], "uint16"),
-    "phi": ("sbuf", [128, 128], "float16"),
+    "phi": ("sbuf", [128, 128], "bfloat16"),
     "tk": ("sbuf", [128, 128], "float16"),
     "cidx": ("sbuf", [128, 1], "int32"),
     "c15": ("sbuf", [128, 1], "int32"),
@@ -25,31 +30,30 @@ SCRATCH = {
     "pcol": ("sbuf", [128, 1], "float32"),
     "gcol": ("sbuf", [128, 1], "float32"),
     "bcol": ("sbuf", [128, 1], "float32"),
-    "y0": ("sbuf", [128, 128], "bfloat16"),
     "u": ("sbuf", [128, 128], "bfloat16"),
     "gx": ("sbuf", [128, 128], "bfloat16"),
+    "k16": ("sbuf", [128, 128], "bfloat16"),
+    "ones": ("sbuf", [128, 128], "bfloat16"),
     "z1": ("sbuf", [128, 128], "bfloat16"),
     "z": ("sbuf", [128, 128], "bfloat16"),
-    "k16": ("sbuf", [128, 128], "float32"),
-    "dumm": ("sbuf", [128, 128], "float32"),
+    "grph": ("sbuf", [128, 128], "float16"),
+    "grpb": ("sbuf", [128, 128], "bfloat16"),
     "pq0": ("sbuf", [128, 128], "int32"),
-    "pq1": ("sbuf", [128, 128], "float32"),
-    "parq": ("sbuf", [128, 128], "float32"),
-    "sel": ("sbuf", [128, 2048], "float16"),
+    "pqm": ("sbuf", [128, 128], "float32"),
     "wrp": ("sbuf", [128, 2048], "bfloat16"),
-    "park": ("sbuf", [128, 2048], "float32"),
-    "key": ("sbuf", [128, 2048], "int32"),
+    "tm": ("sbuf", [128, 2048], "float16"),
+    "hm": ("sbuf", [128, 2048], "bfloat16"),
+    "key": ("sbuf", [128, 2048], "float32"),
     "eq": ("sbuf", [128, 1984], "bfloat16"),
-    "o1": ("sbuf", [128, 128], "float32"),
     "o2": ("sbuf", [128, 128], "float32"),
     "off": ("sbuf", [128, 128], "uint16"),
     "jv": ("sbuf", [128, 1984], "float32"),
     "nv": ("sbuf", [128, WIN], "float32"),
     "ns": ("sbuf", [128, WIN], "float32"),
     "mask": ("sbuf", [128, 64], "float32"),
-    "rst": ("sbuf", [128, 128], "float32"),
-    "m": ("sbuf", [128, 128], "float32"),
-    "sc": ("sbuf", [128, 128], "float32"),
+    "rst": ("sbuf", [128, 128], "float16"),
+    "m": ("sbuf", [128, 128], "float16"),
+    "sc": ("sbuf", [128, 128], "float16"),
     "lst": ("sbuf", [128, 28], "uint16"),
     "ln": ("sbuf", [128, 112], "uint16"),
     "kv_s": ("sbuf", [128, 8192], "bfloat16"),
@@ -57,7 +61,8 @@ SCRATCH = {
     "psa": ("psum", [128, 2048], "float32"),
     "psb": ("psum", [128, 2048], "float32"),
 }
-SEMAPHORES = ["snd1", "snd2a", "snd2b", "gl0", "gl1"] + ["arr%d" % o for o in (1, 2, 3)] + ["e%d" % i for i in range(140)]
+SEMAPHORES = (["snd1a", "snd1b", "snd2a", "snd2b"] + ["arr%d" % o for o in (1, 2, 3)]
+              + ["gl%d%d" % (b, i) for b in (0, 1) for i in (0, 1, 2, 3)] + ["e%d" % i for i in range(130)])
 
 
 def rank_program(g, core, T, topo):
@@ -97,47 +102,55 @@ def rank_program(g, core, T, topo):
     lb[1] = one(Y.dma_start(T.bd[0], part((r + 1) % N)), 16)
     l_par = one(S.dma_start(T.parw[:], T.par[:]), 16)
     lb[3] = one(Y.dma_start(T.bd[2], part((r + 3) % N)), 16)
-    lb[2] = one(S.dma_start(T.bd[1], part((r + 2) % N)), 16)
     l_tok = one(S.dma_start(T.tokd[:], T.tok[:]), 16)
+    lb[2] = one(S.dma_start(T.bd[1], part((r + 2) % N)), 16)
     l_own = one(Y.dma_start(T.own[:], part(r)), 16)
+    l_kv = ev()
+    inc(Y.dma_start(T.kv_s[:, 0:EARLY], T.kv[:, 0:EARLY]), l_kv, 16)
 
     flag = dict(allow_small_or_imprecise_dtypes=True)
-    i_y0 = one(g.iota(T.y0[:], [[-16, 8], [0, 16]], 0, 1, **flag))
     i_c = one(g.iota(T.cidx[:], [[0, 1]], 0, 1))
     i_u = one(g.iota(T.u[:], [[0, 8], [1, 16]], 0, 0, **flag))
+    i_gx = one(g.iota(T.gx[:], [[1, 8], [0, 16]], 0, 0, **flag))
+    i_k = one(g.iota(T.k16[:], [[16, 128]], 0, 0, **flag))
     for o in order:
         d = dst[o]
         rid, pid, _ = topo.addr(d)
         wait(g, lb[o])
-        g.remote_dma(T.land[:, (o - 1) * 128:o * 128], T.bd[o - 1], T.sem["arr%d" % o], T.sem.snd1, pid, rid, topo.mask(core, d))
-    n_snd1 = sum(len(topo.engines(core, dst[o])) for o in order)
-    i_gx = one(g.iota(T.gx[:], [[1, 8], [0, 16]], 0, 0, **flag))
-    i_k = one(g.iota(T.k16[:], [[16, 128]], 2048, 0, **flag))
+        g.remote_dma(T.land[:, (o - 1) * 128:o * 128], T.bd[o - 1], T.sem["arr%d" % o],
+                     T.sem["snd1b" if o == order[-1] else "snd1a"], pid, rid, topo.mask(core, d))
+    n_snd1 = [len(topo.engines(core, dst[o])) for o in order]
     i_jv = one(g.iota(T.jv[:], [[1, 1984]], 64, 0, **flag))
 
-    wait(S, i_y0)
-    e_fill = one(S.activation(T.nv[:, 0:128], T.y0[:], AF.Silu, scale=0.0))
-    n = 128
-    while n < REAL:
-        wait(S, e_fill)
-        w = min(n, REAL - n)
-        e_fill = one(S.activation(T.nv[:, n:n + w], T.nv[:, 0:w], AF.Copy))
-        n = n + w
+    Y.wait_ge(T.sem.snd1a, sum(n_snd1[:-1]))
+    inc(Y.dma_start(T.kv_s[:, EARLY:8192], T.kv[:, EARLY:8192]), l_kv, 16)
 
-    wait(V, i_y0)
-    e_sel = ev()
-    for b in range(16):
-        inc(V.tensor_scalar(T.sel[:, b * 128:(b + 1) * 128], T.y0[:], float(b), None, OP.is_equal), e_sel)
+    e_z0 = one(V.memset(T.nv[:, 0:128], 0.0))
+    e_z2 = one(V.memset(T.nv[:, 256:1216], 0.0))
+    e_one = one(V.memset(T.ones[:], 1.0 / 128))
     wait(V, i_c)
     a = ev()
     inc(V.tensor_scalar(T.c15[:], T.cidx[:], 15, None, OP.bitwise_and), a)
     inc(V.tensor_scalar(T.c4[:], T.cidx[:], 4, None, OP.arith_shift_right), a)
+    e_rst = one(V.memset(T.rst[:], 1.0))
     wait(V, a)
     e_col = ev()
     inc(V.tensor_copy(T.pcol[:], T.c15[:]), e_col)
     inc(V.tensor_copy(T.gcol[:], T.c4[:]), e_col)
+    wait(V, e_rst)
+    e_rst2 = one(V.memset(T.rst[:, 0:128:32], 0.0))
     wait(V, e_col)
     e_b = one(V.tensor_scalar(T.bcol[:], T.pcol[:], -4096.0, 2048.0, OP.mult, OP.add))
+    wait(V, i_u)
+    e_mask = one(V.tensor_scalar(T.mask[:], T.u[:, 0:64], T.pcol[:], None, OP.is_equal))
+    wait(V, i_gx)
+    e_z1 = one(V.tensor_scalar(T.z1[:], T.gx[:], T.gcol[:], 64.0, OP.not_equal, OP.mult))
+    e_grp = ev()
+    inc(V.tensor_scalar(T.grph[:], T.gx[:], T.gcol[:], None, OP.is_equal), e_grp)
+    inc(V.tensor_scalar(T.grpb[:], T.gx[:], T.gcol[:], None, OP.is_equal), e_grp)
+    wait(V, e_z1)
+    e_z = one(V.tensor_tensor(T.z[:], T.z1[:], T.u[:], OP.add))
+
     wait(V, l_par)
     e_hi = one(V.tensor_scalar(T.phi32[:], T.parw[:], 1920, None, OP.bitwise_and))
     e_lo = one(V.tensor_scalar(T.plo32[:], T.parw[:], 127, None, OP.bitwise_and))
@@ -147,89 +160,86 @@ def rank_program(g, core, T, topo):
     e_tk = one(V.tensor_scalar(T.tk[:], T.tokd[:], -2048.0, None, OP.add))
     wait(V, e_lo)
     e_plo = one(V.tensor_copy(T.plo[:], T.plo32[:]))
-    e_p0 = one(V.tensor_scalar(T.pq0[:], T.parw[:], 64.0, 2048.0, OP.is_lt, OP.mult))
-    wait(V, i_u)
-    e_mask = one(V.tensor_scalar(T.mask[:], T.u[:, 0:64], T.pcol[:], None, OP.is_equal))
-    e_rst = one(V.memset(T.rst[:], 1.0))
-    wait(V, e_p0)
-    e_p1 = one(V.tensor_tensor(T.pq1[:], T.pq0[:], T.parw[:], OP.add))
-    wait(V, i_gx)
-    e_z1 = one(V.tensor_scalar(T.z1[:], T.gx[:], T.gcol[:], 64.0, OP.not_equal, OP.mult))
-    wait(V, e_rst)
-    e_rst2 = one(V.memset(T.rst[:, 0:128:32], 0.0))
-    wait(V, e_z1)
-    e_z = one(V.tensor_tensor(T.z[:], T.z1[:], T.u[:], OP.add))
-    wait(V, i_k)
-    e_du = one(V.tensor_scalar(T.dumm[:], T.k16[:], T.pcol[:], None, OP.add))
-    wait(V, e_z)
-    e_wrp = ev()
-    for b in range(16):
-        inc(V.tensor_scalar(T.wrp[:, b * 128:(b + 1) * 128], T.z[:], float(b), None, OP.is_equal), e_wrp)
-    wait(V, e_du, e_p1)
-    e_pq = one(V.tensor_tensor(T.parq[:], T.pq1[:], T.dumm[:], OP.subtract))
-
-    wait(P, e_sel, e_phi)
-    pe_a = []
-    for q in range(4):
-        e = ev()
-        for b in range(4 * q, 4 * q + 4):
-            inc(P.matmul(T.psa[:, b * 128:(b + 1) * 128], T.sel[:, b * 128:(b + 1) * 128], T.phi[:], True, True), e)
-        pe_a.append(e)
-    wait(P, e_tk)
-    pe_b = []
+    e_p0 = one(V.tensor_scalar(T.pq0[:], T.parw[:], 64.0, -2048.0, OP.is_ge, OP.mult))
+    wait(V, e_tk, e_mask, e_phi)
+    e_tm = []
     for q in range(4):
         e = ev()
         for c in range(4 * q, 4 * q + 4):
-            inc(P.matmul(T.psb[:, c * 128:(c + 1) * 128], T.sel[:, c * 128:(c + 1) * 128], T.tk[:], True, True), e)
-        pe_b.append(e)
-
-    wait(S, e_b)
-    e_pk = ev()
+            inc(V.tensor_scalar(T.tm[:, c * 128:(c + 1) * 128], T.tk[:], T.mask[:, c:c + 1], None, OP.mult), e)
+        e_tm.append(e)
+    e_hv = ev()
+    for b in range(HV):
+        inc(V.tensor_scalar(T.hm[:, b:2048:16], T.phi[:], T.mask[:, b:b + 1], None, OP.mult), e_hv)
+    wait(V, e_p0)
+    e_pq = one(V.tensor_tensor(T.pqm[:], T.pq0[:], T.parw[:], OP.add))
+    wait(V, e_z)
+    e_wrp = ev()
     for b in range(16):
-        if b % 4 == 0:
-            wait(S, pe_a[b // 4])
-        inc(S.activation(T.park[:, b:2048:16], T.psa[:, b * 128:(b + 1) * 128], AF.Identity, bias=T.bcol[:]), e_pk)
+        inc(V.tensor_scalar(T.wrp[:, b * 128:(b + 1) * 128], T.z[:], float(b), -8192.0, OP.is_equal, OP.mult), e_wrp)
 
-    wait(V, e_pk)
-    e_key = ev()
+    wait(S, e_z0)
+    e_fill = one(S.activation(T.nv[:, 128:256], T.nv[:, 0:128], AF.Silu))
+    wait(S, e_z2)
+    inc(S.activation(T.nv[:, 1216:REAL], T.nv[:, 256:REAL - 960], AF.Copy), e_fill)
+    wait(S, e_phi, e_mask)
+    e_hm = ev()
+    for b in range(HV, 16):
+        inc(S.activation(T.hm[:, b:2048:16], T.phi[:], AF.Identity, scale=T.mask[:, b:b + 1]), e_hm)
+
+    wait(P, i_k, i_u, e_one)
+    for x in range(len(BATCHES) - 1):
+        a, b = BATCHES[x], BATCHES[x + 1]
+        out = T.psa[:, 512 * x:512 * x + b - a]
+        P.matmul(out, T.ones[:], T.k16[:, a:b], True, False)
+        P.matmul(out, T.u[:], T.ones[:, 0:b - a], False, False)
+    wait(P, e_grp)
     for q in range(4):
-        wait(V, pe_b[q])
-        cs = slice(q * 512, (q + 1) * 512)
-        inc(V.tensor_tensor(T.key[:, cs], T.psb[:, cs], T.park[:, cs], OP.add), e_key)
-
+        wait(P, e_tm[q])
+        P.matmul(T.psb[:, q * 512:(q + 1) * 512], T.grph[:], T.tm[:, q * 512:(q + 1) * 512], True, False)
+    wait(P, e_hm, e_hv)
+    pe_k = [one(P.matmul(T.psb[:, q * 512:(q + 1) * 512], T.grpb[:], T.hm[:, q * 512:(q + 1) * 512], False, True)) for q in range(4)]
+    wait(S, e_b)
+    e_key = []
+    for q in range(4):
+        wait(S, pe_k[q])
+        e_key.append(one(S.activation(T.key[:, q * 512:(q + 1) * 512], T.psb[:, q * 512:(q + 1) * 512], AF.Identity, bias=T.bcol[:])))
     wait(S, e_fill)
     e_fill2 = one(S.activation(T.ns[:, 0:REAL], T.nv[:, 0:REAL], AF.Copy))
 
     wait(V, l_own)
+    run = T.psa[:, 1536:1664]
     src = T.own[:]
     for n, o in enumerate(order):
         sender = T.cores[(r - o) % N]
         V.wait_ge(T.sem["arr%d" % o], len(topo.engines(sender, core)))
-        e = one(V.tensor_tensor(T.mx[:, n * 128:(n + 1) * 128], src, T.land[:, (o - 1) * 128:o * 128], OP.max))
+        out = run if n < 2 else T.mx[:]
+        e = one(V.tensor_tensor(out, src, T.land[:, (o - 1) * 128:o * 128], OP.max))
         wait(V, e)
-        src = T.mx[:, n * 128:(n + 1) * 128]
-    e_tgt = one(V.tensor_scalar(T.tgt[:], src, 4095, None, OP.bitwise_and))
-    wait(V, e_tgt, e_key, e_plo)
+        src = out
+    e_tgt = one(V.tensor_scalar(T.tgt[:], T.mx[:], 4095, None, OP.bitwise_and))
+    wait(V, e_tgt, e_plo)
 
-    def match(a, b):
+    def match(x):
+        a, b = BATCHES[x], BATCHES[x + 1]
+        wait(V, *[e_key[q] for q in range(4) if q * 32 < b and a < (q + 1) * 32])
         return one(V.tensor_tensor(T.eq[:, (a - 4) * 16:(b - 4) * 16], T.tgt[:, 0:128].indirect(T.plo[:, a:b]),
                                    T.key[:, a * 16:b * 16], OP.is_equal))
 
-    def gather_bits(a, b, bank):
-        e = ev()
-        for x in range(16):
-            inc(P.matmul(T.psa[:, 512 * bank:512 * bank + b - a], T.wrp[:, x * 128:(x + 1) * 128],
-                         T.eq[:, (a - 4) * 16 + x:(b - 4) * 16:16], x == 0, x == 15), e)
-        return e
+    def gather_bits(x, e_m):
+        a, b = BATCHES[x], BATCHES[x + 1]
+        wait(P, e_m)
+        for i in range(16):
+            ins = P.matmul(T.psa[:, 512 * x:512 * x + b - a], T.wrp[:, i * 128:(i + 1) * 128],
+                           T.eq[:, (a - 4) * 16 + i:(b - 4) * 16:16], False, i == 15)
+        return one(ins)
 
-    def offsets(a, b, bank, e_ok):
-        cs = slice(a, b)
+    def offsets(x, e_ok):
+        a, b = BATCHES[x], BATCHES[x + 1]
         wait(V, e_ok)
-        e = one(V.tensor_tensor(T.o1[:, cs], T.psa[:, 512 * bank:512 * bank + b - a], T.parq[:, cs], OP.mult))
+        e = one(V.tensor_tensor(T.o2[:, a:b], T.psa[:, 512 * x:512 * x + b - a], T.pqm[:, a:b], OP.max))
         wait(V, e)
-        e = one(V.tensor_tensor(T.o2[:, cs], T.o1[:, cs], T.dumm[:, cs], OP.add))
-        wait(V, e)
-        return one(V.tensor_copy(T.off[:, cs], T.o2[:, cs]))
+        return one(V.tensor_scalar(T.off[:, a:b], T.o2[:, a:b], 2048.0, None, OP.add))
 
     def scatter_v(a, b):
         return one(V.tensor_copy(T.nv[:, 0:WIN].indirect(T.off[:, a:b]), T.jv[:, (a - 4) * 16:(b - 4) * 16]))
@@ -237,28 +247,32 @@ def rank_program(g, core, T, topo):
     def scatter_s(a, b):
         return one(S.activation(T.ns[:, 0:WIN].indirect(T.off[:, a:b]), T.jv[:, (a - 4) * 16:(b - 4) * 16], AF.Silu))
 
-    A0, A1, A2, B1, B2 = 4, 28, 66, 98, 128
-    m_a = match(A0, A2)
-    m_b1 = match(A2, 106)
-    wait(P, e_wrp, e_pk, m_a)
-    ok_a = gather_bits(A0, A2, 0)
-    wait(V, e_pq)
-    off_a = offsets(A0, A2, 0, ok_a)
-    m_b2 = match(106, B2)
-    wait(P, m_b1, m_b2)
-    ok_b = gather_bits(A2, B2, 1)
-    wait(S, e_fill2, i_jv, off_a)
-    s_a = scatter_s(A1, A2)
-    wait(V, e_fill2, i_jv, off_a)
-    v_a = scatter_v(A0, A1)
-    off_b = offsets(A2, B2, 1, ok_b)
-    wait(S, off_b, s_a)
-    s_b = scatter_s(B1, B2)
-    wait(V, off_b, v_a)
-    v_b = scatter_v(A2, B1)
+    wait(P, e_wrp)
+    wait(S, e_fill2, i_jv)
+    last = {"s": None, "v": None}
 
-    Y.wait_ge(T.sem.snd1, n_snd1)
-    l_kv = one(Y.dma_start(T.kv_s[:], T.kv[:]), 16)
+    def scatters(x, e_off):
+        a, b = BATCHES[x], BATCHES[x + 1]
+        sa, sb = S_PART[x]
+        wait(S, e_off)
+        if last["s"]:
+            wait(S, last["s"])
+        last["s"] = scatter_s(sa, sb)
+        if a < sa:
+            wait(V, e_off)
+            if last["v"]:
+                wait(V, last["v"])
+            else:
+                wait(V, e_fill2, i_jv)
+            last["v"] = scatter_v(a, sa)
+
+    ok0 = gather_bits(0, match(0))
+    ok1 = gather_bits(1, match(1))
+    wait(V, e_pq)
+    scatters(0, offsets(0, ok0))
+    ok2 = gather_bits(2, match(2))
+    scatters(1, offsets(1, ok1))
+    scatters(2, offsets(2, ok2))
 
     ys = [ev() for i in range(N)]
     yv = [ev() for i in range(N)]
@@ -274,6 +288,7 @@ def rank_program(g, core, T, topo):
         e = ev()
         if d == 1:
             inc(V.tensor_tensor(T.m[:, 0:128:2], T.nv[:, 2048:2112], T.mask[:], OP.mult), e)
+            wait(V, last["s"])
             inc(V.tensor_tensor(T.m[:, 1:128:2], T.ns[:, 2048:2112], T.mask[:], OP.mult), e)
         else:
             cs = slice(4 * (d - 2), 4 * (d - 1))
@@ -286,20 +301,17 @@ def rank_program(g, core, T, topo):
         wait(V, e)
         return e
 
-    wait(V, v_b, s_b, e_mask, e_rst2)
+    wait(V, last["v"], e_rst2)
     e_l = {}
     for d in range(1, 8):
         e_l[d] = step(d)
 
     mask = topo.mask(core, dst[1]) & topo.mask(core, dst[2]) & topo.mask(core, dst[3])
     bits = bin(mask).count("1")
-    ids = []
-    for o in order:
-        rid, pid, _ = topo.addr(dst[o])
-        ids.append(DstId(rid=rid, pnc=pid))
-    for b, (d, c0, c1) in enumerate(((4, 0, 16), (7, 16, 28))):
+    ids = [DstId(rid=topo.addr(dst[o])[0], pnc=topo.addr(dst[o])[1]) for o in order]
+    for b, (d, c0, c1) in enumerate(LISTS):
         wait(g, e_l[d])
-        g.remote_dma_fused([RemoteDMATransfer(dst_ids=ids, dma_engine_mask=mask, remote_sem=T.sem["gl%d" % b],
+        g.remote_dma_fused([RemoteDMATransfer(dst_ids=ids, dma_engine_mask=mask, remote_sem=T.sem["gl%d%d" % (b, r)],
                                               srcs=[T.lst[:, c0:c1]], dsts=[T.ln[:, r * 28 + c0:r * 28 + c1] for _ in ids])],
                            local_sem=T.sem["snd2a" if b == 0 else "snd2b"])
 
@@ -312,36 +324,30 @@ def rank_program(g, core, T, topo):
         else:
             inc(S.activation(out, win, AF.Copy), ys[i])
 
-    def arrived(q, b):
-        q.wait_ge(T.sem["gl%d" % b], bits * (N - 1))
-
-    others = [i for i in range(N) if i != r]
-    wait(V, e_zero)
-    for d in range(1, 5):
+    for d in range(1, 7):
         wait(S, e_l[d])
         pick(1, r, d)
-    for d in range(5, 8):
-        pick(0, r, d)
+    wait(V, e_zero)
+    pick(0, r, 7)
     wait(Y, yv[r], ys[r], e_root)
     stores = [one(Y.dma_start(T.y[:, r * 512:(r + 1) * 512], T.yb[:, r * 512:(r + 1) * 512]), 16)]
-    arrived(V, 0)
-    arrived(S, 0)
-    for i in others:
-        pick(0, i, 1)
-        pick(0, i, 2)
-        pick(1, i, 3)
-        pick(1, i, 4)
-    arrived(V, 1)
-    arrived(S, 1)
-    for n, i in enumerate(others):
-        pick(0, i, 5)
-        pick(n % 2, i, 6)
-        pick(1, i, 7)
-    for i in others:
+    cut = LISTS[0][0]
+    for b, ds in enumerate((range(1, cut + 1), range(cut + 1, 8))):
+        n = 0
+        for o in order:
+            i = (r - o) % N
+            V.wait_ge(T.sem["gl%d%d" % (b, i)], bits)
+            S.wait_ge(T.sem["gl%d%d" % (b, i)], bits)
+            for d in ds:
+                pick(n % 2, i, d)
+                n = n + 1
+    for o in order:
+        i = (r - o) % N
         wait(Y, yv[i], ys[i])
         stores.append(one(Y.dma_start(T.y[:, i * 512:(i + 1) * 512], T.yb[:, i * 512:(i + 1) * 512]), 16))
     for e in stores:
         wait(Y, e)
+    g.wait_ge(T.sem.snd1b, n_snd1[-1])
     g.wait_ge(T.sem.snd2a, bits)
     g.wait_ge(T.sem.snd2b, bits)
     for e in list(count):

@@ -3,13 +3,16 @@ from concourse.mybir import AluOpType, ActivationFunctionType
 
 OP = AluOpType
 AF = ActivationFunctionType
-REAL = 2112
+NONE = 2112
+REAL = NONE + 1
 WIN = REAL + 1984
+KW = 2128
 EARLY = 512
-BATCHES = (4, 32, 74, 128)
-S_PART = ((4, 32), (50, 74), (102, 128))
-HV = 4
+BATCHES = (4, 22, 64, 128)
+S_PART = ((4, 22), (42, 64), (96, 128))
 LISTS = ((4, 0, 16), (7, 16, 28))
+BIG = 131072.0
+LIFT = 4096.0
 
 SCRATCH = {
     "bd": ("dram", [3, 128, 128], "int32"),
@@ -17,6 +20,7 @@ SCRATCH = {
     "land": ("sbuf", [128, 384], "int32"),
     "mx": ("sbuf", [128, 128], "int32"),
     "tgt": ("sbuf", [128, 128], "int32"),
+    "tgtf": ("sbuf", [128, 128], "float32"),
     "parw": ("sbuf", [128, 128], "int32"),
     "tokd": ("sbuf", [128, 128], "int32"),
     "plo32": ("sbuf", [128, 128], "int32"),
@@ -24,39 +28,40 @@ SCRATCH = {
     "plo": ("sbuf", [128, 128], "uint16"),
     "phi": ("sbuf", [128, 128], "bfloat16"),
     "tk": ("sbuf", [128, 128], "float16"),
-    "cidx": ("sbuf", [128, 1], "int32"),
-    "c15": ("sbuf", [128, 1], "int32"),
-    "c4": ("sbuf", [128, 1], "int32"),
-    "pcol": ("sbuf", [128, 1], "float32"),
+    "pb": ("sbuf", [128, 16], "int32"),
+    "bits": ("sbuf", [128, 24], "int32"),
+    "gi": ("sbuf", [128, 1], "int32"),
+    "mask": ("sbuf", [128, 24], "float32"),
     "gcol": ("sbuf", [128, 1], "float32"),
-    "bcol": ("sbuf", [128, 1], "float32"),
+    "ccol": ("sbuf", [128, 1], "float32"),
+    "lcol": ("sbuf", [128, 1], "float32"),
     "u": ("sbuf", [128, 128], "bfloat16"),
     "gx": ("sbuf", [128, 128], "bfloat16"),
     "k16": ("sbuf", [128, 128], "bfloat16"),
-    "ones": ("sbuf", [128, 128], "bfloat16"),
-    "z1": ("sbuf", [128, 128], "bfloat16"),
-    "z": ("sbuf", [128, 128], "bfloat16"),
-    "grph": ("sbuf", [128, 128], "float16"),
-    "grpb": ("sbuf", [128, 128], "bfloat16"),
-    "pq0": ("sbuf", [128, 128], "int32"),
-    "pqm": ("sbuf", [128, 128], "float32"),
-    "wrp": ("sbuf", [128, 2048], "bfloat16"),
-    "tm": ("sbuf", [128, 2048], "float16"),
-    "hm": ("sbuf", [128, 2048], "bfloat16"),
+    "wx": ("sbuf", [128, 144], "bfloat16"),
+    "x32": ("sbuf", [128, 128], "bfloat16"),
+    "ones": ("sbuf", [128, 512], "bfloat16"),
+    "bl": ("sbuf", [128, 128], "bfloat16"),
+    "gt": ("sbuf", [128, 512], "float16"),
+    "gp": ("sbuf", [128, 512], "bfloat16"),
+    "tm": ("sbuf", [128, 512], "float16"),
+    "hm": ("sbuf", [128, 512], "bfloat16"),
+    "wsel": ("sbuf", [128, 144], "bfloat16"),
+    "cc0": ("sbuf", [128, 128], "bfloat16"),
+    "cc": ("sbuf", [128, 128], "bfloat16"),
     "key": ("sbuf", [128, 2048], "float32"),
+    "tg": ("sbuf", [128, 1984], "float32"),
     "eq": ("sbuf", [128, 1984], "bfloat16"),
     "o2": ("sbuf", [128, 128], "float32"),
     "off": ("sbuf", [128, 128], "uint16"),
     "jv": ("sbuf", [128, 1984], "float32"),
     "nv": ("sbuf", [128, WIN], "float32"),
     "ns": ("sbuf", [128, WIN], "float32"),
-    "mask": ("sbuf", [128, 64], "float32"),
-    "rst": ("sbuf", [128, 128], "float16"),
-    "m": ("sbuf", [128, 128], "float16"),
-    "sc": ("sbuf", [128, 128], "float16"),
+    "m": ("sbuf", [128, 128], "float32"),
+    "sc": ("sbuf", [128, 128], "float32"),
     "lst": ("sbuf", [128, 28], "uint16"),
     "ln": ("sbuf", [128, 112], "uint16"),
-    "kv_s": ("sbuf", [128, 8192], "bfloat16"),
+    "kv_s": ("sbuf", [128, 4 * KW], "bfloat16"),
     "yb": ("sbuf", [128, 2048], "bfloat16"),
     "psa": ("psum", [128, 2048], "float32"),
     "psb": ("psum", [128, 2048], "float32"),
@@ -109,10 +114,9 @@ def rank_program(g, core, T, topo):
     inc(Y.dma_start(T.kv_s[:, 0:EARLY], T.kv[:, 0:EARLY]), l_kv, 16)
 
     flag = dict(allow_small_or_imprecise_dtypes=True)
-    i_c = one(g.iota(T.cidx[:], [[0, 1]], 0, 1))
-    i_u = one(g.iota(T.u[:], [[0, 8], [1, 16]], 0, 0, **flag))
-    i_gx = one(g.iota(T.gx[:], [[1, 8], [0, 16]], 0, 0, **flag))
-    i_k = one(g.iota(T.k16[:], [[16, 128]], 0, 0, **flag))
+    i_pb = one(g.iota(T.pb[:], [[-1, 16]], 0, 1))
+    i_gx = one(g.iota(T.gx[:], [[16, 8], [0, 16]], 0, 0, **flag))
+    i_u = one(g.iota(T.u[:], [[0, 8], [1, 16]], 1, 0, **flag))
     for o in order:
         d = dst[o]
         rid, pid, _ = topo.addr(d)
@@ -120,92 +124,104 @@ def rank_program(g, core, T, topo):
         g.remote_dma(T.land[:, (o - 1) * 128:o * 128], T.bd[o - 1], T.sem["arr%d" % o],
                      T.sem["snd1b" if o == order[-1] else "snd1a"], pid, rid, topo.mask(core, d))
     n_snd1 = [len(topo.engines(core, dst[o])) for o in order]
-    i_jv = one(g.iota(T.jv[:], [[1, 1984]], 64, 0, **flag))
+    i_k = one(g.iota(T.k16[:], [[16, 128]], 2048, 0, **flag))
+    i_w = one(g.iota(T.wx[:], [[1, 144]], -15, 0, **flag))
+    i_x = one(g.iota(T.x32[:], [[0, 4], [1, 32]], 0, 0, **flag))
+    cut0 = (S_PART[1][0] - 4) * 16
+    i_j0 = one(g.iota(T.jv[:, 0:cut0], [[-1, cut0]], NONE - 64, 0, **flag))
+    i_j1 = one(g.iota(T.jv[:, cut0:1984], [[-1, 1984 - cut0]], NONE - 64 - cut0, 0, **flag))
+    i_kz = ev()
+    for i in range(N):
+        inc(g.iota(T.kv_s[:, i * KW + 2048:(i + 1) * KW], [[0, KW - 2048]], 0, 0, **flag), i_kz)
 
     Y.wait_ge(T.sem.snd1a, sum(n_snd1[:-1]))
-    inc(Y.dma_start(T.kv_s[:, EARLY:8192], T.kv[:, EARLY:8192]), l_kv, 16)
+    inc(Y.dma_start(T.kv_s[:, EARLY:2048], T.kv[:, EARLY:2048]), l_kv, 16)
+    for i in range(1, N):
+        inc(Y.dma_start(T.kv_s[:, i * KW:i * KW + 2048], T.kv[:, i * 2048:(i + 1) * 2048]), l_kv, 16)
 
-    e_z0 = one(V.memset(T.nv[:, 0:128], 0.0))
-    e_z2 = one(V.memset(T.nv[:, 256:1216], 0.0))
+    e_z0 = one(V.memset(T.ns[:, 0:160], 0.0))
     e_one = one(V.memset(T.ones[:], 1.0 / 128))
-    wait(V, i_c)
+    wait(V, i_pb)
     a = ev()
-    inc(V.tensor_scalar(T.c15[:], T.cidx[:], 15, None, OP.bitwise_and), a)
-    inc(V.tensor_scalar(T.c4[:], T.cidx[:], 4, None, OP.arith_shift_right), a)
-    e_rst = one(V.memset(T.rst[:], 1.0))
+    inc(V.tensor_scalar(T.bits[:, 0:16], T.pb[:], 15, None, OP.bitwise_and), a)
+    inc(V.tensor_scalar(T.bits[:, 16:20], T.pb[:, 0:4], 3, None, OP.bitwise_and), a)
+    inc(V.tensor_scalar(T.bits[:, 20:24], T.pb[:, 0:16:4], 12, None, OP.bitwise_and), a)
+    inc(V.tensor_scalar(T.gi[:], T.pb[:, 0:1], 112, None, OP.bitwise_and), a)
     wait(V, a)
     e_col = ev()
-    inc(V.tensor_copy(T.pcol[:], T.c15[:]), e_col)
-    inc(V.tensor_copy(T.gcol[:], T.c4[:]), e_col)
-    wait(V, e_rst)
-    e_rst2 = one(V.memset(T.rst[:, 0:128:32], 0.0))
-    wait(V, e_col)
-    e_b = one(V.tensor_scalar(T.bcol[:], T.pcol[:], -4096.0, 2048.0, OP.mult, OP.add))
+    inc(V.tensor_scalar(T.mask[:], T.bits[:], 0.0, None, OP.is_equal), e_col)
+    inc(V.tensor_copy(T.gcol[:], T.gi[:]), e_col)
+    wait(V, i_gx, e_col)
+    e_g = ev()
+    for q in range(4):
+        inc(V.tensor_scalar(T.gp[:, q * 128:(q + 1) * 128], T.gx[:], T.gcol[:], T.mask[:, 16 + q:17 + q], OP.is_equal, OP.mult), e_g)
     wait(V, i_u)
-    e_mask = one(V.tensor_scalar(T.mask[:], T.u[:, 0:64], T.pcol[:], None, OP.is_equal))
-    wait(V, i_gx)
-    e_z1 = one(V.tensor_scalar(T.z1[:], T.gx[:], T.gcol[:], 64.0, OP.not_equal, OP.mult))
-    e_grp = ev()
-    inc(V.tensor_scalar(T.grph[:], T.gx[:], T.gcol[:], None, OP.is_equal), e_grp)
-    inc(V.tensor_scalar(T.grpb[:], T.gx[:], T.gcol[:], None, OP.is_equal), e_grp)
-    wait(V, e_z1)
-    e_z = one(V.tensor_tensor(T.z[:], T.z1[:], T.u[:], OP.add))
+    e_bl = one(V.tensor_scalar(T.bl[:], T.u[:], -4096.0, 4096.0 + 2048.0, OP.mult, OP.add))
 
     wait(V, l_par)
     e_hi = one(V.tensor_scalar(T.phi32[:], T.parw[:], 1920, None, OP.bitwise_and))
     e_lo = one(V.tensor_scalar(T.plo32[:], T.parw[:], 127, None, OP.bitwise_and))
     wait(V, e_hi)
     e_phi = one(V.tensor_scalar(T.phi[:], T.phi32[:], 32.0, None, OP.mult))
+    e_gt = ev()
+    for q in range(4):
+        inc(V.tensor_scalar(T.gt[:, q * 128:(q + 1) * 128], T.gx[:], T.gcol[:], T.mask[:, 20 + q:21 + q], OP.is_equal, OP.mult), e_gt)
+    wait(V, e_phi)
+    e_hm = ev()
+    for s in range(4):
+        inc(V.tensor_scalar(T.hm[:, s:512:4], T.phi[:], T.mask[:, 20 + s:21 + s], None, OP.mult), e_hm)
     wait(V, l_tok)
     e_tk = one(V.tensor_scalar(T.tk[:], T.tokd[:], -2048.0, None, OP.add))
     wait(V, e_lo)
     e_plo = one(V.tensor_copy(T.plo[:], T.plo32[:]))
-    e_p0 = one(V.tensor_scalar(T.pq0[:], T.parw[:], 64.0, -2048.0, OP.is_ge, OP.mult))
-    wait(V, e_tk, e_mask, e_phi)
-    e_tm = []
+    wait(V, e_tk)
+    e_tm = ev()
     for q in range(4):
-        e = ev()
-        for c in range(4 * q, 4 * q + 4):
-            inc(V.tensor_scalar(T.tm[:, c * 128:(c + 1) * 128], T.tk[:], T.mask[:, c:c + 1], None, OP.mult), e)
-        e_tm.append(e)
-    e_hv = ev()
-    for b in range(HV):
-        inc(V.tensor_scalar(T.hm[:, b:2048:16], T.phi[:], T.mask[:, b:b + 1], None, OP.mult), e_hv)
-    wait(V, e_p0)
-    e_pq = one(V.tensor_tensor(T.pqm[:], T.pq0[:], T.parw[:], OP.add))
-    wait(V, e_z)
-    e_wrp = ev()
-    for b in range(16):
-        inc(V.tensor_scalar(T.wrp[:, b * 128:(b + 1) * 128], T.z[:], float(b), -8192.0, OP.is_equal, OP.mult), e_wrp)
+        inc(V.tensor_scalar(T.tm[:, q * 128:(q + 1) * 128], T.tk[:], T.mask[:, 16 + q:17 + q], None, OP.mult), e_tm)
+    e_cl = ev()
+    inc(V.tensor_scalar(T.ccol[:], T.bits[:, 0:1], -2.0 * BIG, -BIG, OP.mult, OP.add), e_cl)
+    inc(V.tensor_scalar(T.lcol[:], T.bits[:, 0:1], -2.0 * LIFT, 30.0 * LIFT + NONE + 0.25, OP.mult, OP.add), e_cl)
+    e_fill = one(V.memset(T.nv[:, 0:REAL], 0.0))
+    wait(V, i_w)
+    e_wsel = one(V.tensor_scalar(T.wsel[:], T.wx[:], T.gcol[:], -8192.0, OP.is_equal, OP.mult))
 
     wait(S, e_z0)
-    e_fill = one(S.activation(T.nv[:, 128:256], T.nv[:, 0:128], AF.Silu))
-    wait(S, e_z2)
-    inc(S.activation(T.nv[:, 1216:REAL], T.nv[:, 256:REAL - 960], AF.Copy), e_fill)
-    wait(S, e_phi, e_mask)
-    e_hm = ev()
-    for b in range(HV, 16):
-        inc(S.activation(T.hm[:, b:2048:16], T.phi[:], AF.Identity, scale=T.mask[:, b:b + 1]), e_hm)
+    e_s = one(S.activation(T.ns[:, 160:320], T.ns[:, 0:160], AF.Silu))
+    wait(S, e_s)
+    e_s = one(S.activation(T.ns[:, 320:640], T.ns[:, 0:320], AF.Copy))
+    wait(S, e_s)
+    e_s = one(S.activation(T.ns[:, 640:1280], T.ns[:, 0:640], AF.Copy))
+    wait(S, e_s)
+    e_s2 = one(S.activation(T.ns[:, 1280:REAL], T.ns[:, 0:REAL - 1280], AF.Copy))
 
-    wait(P, i_k, i_u, e_one)
+    wait(P, e_one, e_bl)
+    for q in range(4):
+        P.matmul(T.psb[:, q * 512:(q + 1) * 512], T.bl[:], T.ones[:], True, False)
+    wait(P, e_g, e_hm)
+    pe_k = []
+    for q in range(4):
+        for s in range(4):
+            P.matmul(T.psb[:, q * 512 + s:(q + 1) * 512:4], T.gp[:, s * 128:(s + 1) * 128], T.hm[:, q * 128:(q + 1) * 128], False, False)
+        if q == 0:
+            wait(P, e_gt, e_tm)
+        pe_k.append(one(P.matmul(T.psb[:, q * 512:(q + 1) * 512], T.gt[:, q * 128:(q + 1) * 128], T.tm[:], False, True)))
+    wait(P, i_k, i_u)
     for x in range(len(BATCHES) - 1):
         a, b = BATCHES[x], BATCHES[x + 1]
         out = T.psa[:, 512 * x:512 * x + b - a]
-        P.matmul(out, T.ones[:], T.k16[:, a:b], True, False)
+        P.matmul(out, T.ones[:, 0:128], T.k16[:, a:b], True, False)
         P.matmul(out, T.u[:], T.ones[:, 0:b - a], False, False)
-    wait(P, e_grp)
-    for q in range(4):
-        wait(P, e_tm[q])
-        P.matmul(T.psb[:, q * 512:(q + 1) * 512], T.grph[:], T.tm[:, q * 512:(q + 1) * 512], True, False)
-    wait(P, e_hm, e_hv)
-    pe_k = [one(P.matmul(T.psb[:, q * 512:(q + 1) * 512], T.grpb[:], T.hm[:, q * 512:(q + 1) * 512], False, True)) for q in range(4)]
-    wait(S, e_b)
+    a3 = BATCHES[-2]
     e_key = []
     for q in range(4):
         wait(S, pe_k[q])
-        e_key.append(one(S.activation(T.key[:, q * 512:(q + 1) * 512], T.psb[:, q * 512:(q + 1) * 512], AF.Identity, bias=T.bcol[:])))
-    wait(S, e_fill)
-    e_fill2 = one(S.activation(T.ns[:, 0:REAL], T.nv[:, 0:REAL], AF.Copy))
+        hi = min((q + 1) * 512, a3 * 16)
+        if hi > q * 512:
+            e_key.append(one(S.activation(T.key[:, q * 512:hi], T.psb[:, q * 512:hi], AF.Copy)))
+        else:
+            e_key.append(pe_k[q])
+    wait(S, i_x, e_cl)
+    e_c0 = one(S.activation(T.cc0[:], T.x32[:], AF.Identity, bias=T.ccol[:], scale=BIG))
 
     wait(V, l_own)
     run = T.psa[:, 1536:1664]
@@ -230,16 +246,16 @@ def rank_program(g, core, T, topo):
         a, b = BATCHES[x], BATCHES[x + 1]
         wait(P, e_m)
         for i in range(16):
-            ins = P.matmul(T.psa[:, 512 * x:512 * x + b - a], T.wrp[:, i * 128:(i + 1) * 128],
+            ins = P.matmul(T.psa[:, 512 * x:512 * x + b - a], T.wsel[:, 15 - i:143 - i],
                            T.eq[:, (a - 4) * 16 + i:(b - 4) * 16:16], False, i == 15)
         return one(ins)
 
     def offsets(x, e_ok):
         a, b = BATCHES[x], BATCHES[x + 1]
         wait(V, e_ok)
-        e = one(V.tensor_tensor(T.o2[:, a:b], T.psa[:, 512 * x:512 * x + b - a], T.pqm[:, a:b], OP.max))
+        e = one(V.tensor_tensor(T.o2[:, a:b], T.psa[:, 512 * x:512 * x + b - a], T.parw[:, a:b], OP.max))
         wait(V, e)
-        return one(V.tensor_scalar(T.off[:, a:b], T.o2[:, a:b], 2048.0, None, OP.add))
+        return one(V.tensor_copy(T.off[:, a:b], T.o2[:, a:b]))
 
     def scatter_v(a, b):
         return one(V.tensor_copy(T.nv[:, 0:WIN].indirect(T.off[:, a:b]), T.jv[:, (a - 4) * 16:(b - 4) * 16]))
@@ -247,8 +263,7 @@ def rank_program(g, core, T, topo):
     def scatter_s(a, b):
         return one(S.activation(T.ns[:, 0:WIN].indirect(T.off[:, a:b]), T.jv[:, (a - 4) * 16:(b - 4) * 16], AF.Silu))
 
-    wait(P, e_wrp)
-    wait(S, e_fill2, i_jv)
+    wait(P, e_wsel)
     last = {"s": None, "v": None}
 
     def scatters(x, e_off):
@@ -257,54 +272,79 @@ def rank_program(g, core, T, topo):
         wait(S, e_off)
         if last["s"]:
             wait(S, last["s"])
+        else:
+            wait(S, e_s2, i_j0)
+        if x == 1:
+            wait(S, i_j1)
         last["s"] = scatter_s(sa, sb)
         if a < sa:
             wait(V, e_off)
             if last["v"]:
                 wait(V, last["v"])
             else:
-                wait(V, e_fill2, i_jv)
+                wait(V, e_fill, i_j0)
+            if x == 2:
+                wait(V, i_j1)
             last["v"] = scatter_v(a, sa)
 
+    e_tf = one(V.tensor_copy(T.tgtf[:], T.tgt[:]))
+    wait(S, e_tf, e_plo)
+    c3, d3 = (a3 - 4) * 16, 1984
+    e_tg = one(S.activation(T.tg[:, c3:d3], T.tgtf[:, 0:128].indirect(T.plo[:, a3:128]), AF.Copy))
     ok0 = gather_bits(0, match(0))
     ok1 = gather_bits(1, match(1))
-    wait(V, e_pq)
+    wait(V, e_c0)
+    e_cc = one(V.tensor_scalar(T.cc[:], T.cc0[:], LIFT, None, OP.min))
     scatters(0, offsets(0, ok0))
-    ok2 = gather_bits(2, match(2))
+    wait(V, e_tg, *[e_key[q] for q in range(4)])
+    e = ev()
+    mid = c3
+    while mid < d3:
+        end = min(d3, (mid + 64) // 512 * 512 + 512 - 64)
+        inc(V.tensor_tensor(T.eq[:, mid:end], T.tg[:, mid:end], T.psb[:, mid + 64:end + 64], OP.is_equal), e)
+        mid = end
+    ok2 = gather_bits(2, e)
     scatters(1, offsets(1, ok1))
     scatters(2, offsets(2, ok2))
 
     ys = [ev() for i in range(N)]
     yv = [ev() for i in range(N)]
-    wait(S, l_kv)
     e_root = ev()
-    for i in range(N):
-        inc(S.activation(T.yb[:, i * 512:(i + 1) * 512:8], T.kv_s[:, i * 2048:i * 2048 + 64], AF.Copy), e_root)
-    wait(S, e_root)
-    e_zero = one(S.activation(T.kv_s[:, 0:8192:2048], T.kv_s[:, 0:8192:2048], AF.Copy, scale=0.0))
-    wait(S, e_zero)
 
-    def step(d):
-        e = ev()
-        if d == 1:
-            inc(V.tensor_tensor(T.m[:, 0:128:2], T.nv[:, 2048:2112], T.mask[:], OP.mult), e)
-            wait(V, last["s"])
-            inc(V.tensor_tensor(T.m[:, 1:128:2], T.ns[:, 2048:2112], T.mask[:], OP.mult), e)
+    def pick(q, i, d):
+        lists = T.lst[:, 4 * (d - 1):4 * d] if i == r else T.ln[:, i * 28 + 4 * (d - 1):i * 28 + 4 * d]
+        out = T.yb[:, i * 512 + d:(i + 1) * 512:8]
+        win = T.kv_s[:, i * KW:i * KW + REAL].indirect(lists)
+        if q == 0:
+            inc(V.tensor_copy(out, win), yv[i])
         else:
-            cs = slice(4 * (d - 2), 4 * (d - 1))
-            inc(V.tensor_tensor(T.m[:, 0:128:2], T.nv[:, 0:REAL].indirect(T.lst[:, cs]), T.mask[:], OP.mult), e)
-            inc(V.tensor_tensor(T.m[:, 1:128:2], T.ns[:, 0:REAL].indirect(T.lst[:, cs]), T.mask[:], OP.mult), e)
-        wait(V, e)
-        e = one(V.tensor_tensor_scan(T.sc[:], T.rst[:], T.m[:], 0.0, OP.mult, OP.add))
-        wait(V, e)
-        e = one(V.tensor_scalar(T.lst[:, 4 * (d - 1):4 * d], T.sc[:, 31:128:32], 0.25, None, OP.add))
-        wait(V, e)
-        return e
+            inc(S.activation(out, win, AF.Copy), ys[i])
 
-    wait(V, last["v"], e_rst2)
+    wait(V, last["v"], e_cc, e_cl)
+    wait(S, last["s"])
     e_l = {}
     for d in range(1, 8):
-        e_l[d] = step(d)
+        if d == 1:
+            e_a = one(V.tensor_copy(T.m[:, 0:128:2], T.nv[:, 0:64]))
+            e_b = one(S.activation(T.m[:, 1:128:2], T.ns[:, 0:64], AF.Copy))
+        else:
+            lists = T.lst[:, 4 * (d - 2):4 * (d - 1)]
+            wait(S, e_l[d - 1])
+            e_a = one(V.tensor_copy(T.m[:, 0:128:2], T.nv[:, 0:REAL].indirect(lists)))
+            e_b = one(S.activation(T.m[:, 1:128:2], T.ns[:, 0:REAL].indirect(lists), AF.Copy))
+        wait(V, e_a, e_b)
+        e = one(V.tensor_tensor_scan(T.sc[:], T.cc[:], T.m[:], 0.0, OP.add, OP.max))
+        wait(V, e)
+        e_l[d] = one(V.tensor_scalar(T.lst[:, 4 * (d - 1):4 * d], T.sc[:, 31:128:32], -1.0, T.lcol[:], OP.mult, OP.add))
+        wait(V, e_l[d])
+        if d == 4:
+            wait(S, l_kv, i_kz)
+        if d >= 4:
+            for x in (d - 4, d):
+                if x < N:
+                    inc(S.activation(T.yb[:, x * 512:(x + 1) * 512:8], T.kv_s[:, x * KW:x * KW + 64], AF.Copy), e_root)
+                elif x >= 5:
+                    pick(1, r, x - 4)
 
     mask = topo.mask(core, dst[1]) & topo.mask(core, dst[2]) & topo.mask(core, dst[3])
     bits = bin(mask).count("1")
@@ -315,20 +355,10 @@ def rank_program(g, core, T, topo):
                                               srcs=[T.lst[:, c0:c1]], dsts=[T.ln[:, r * 28 + c0:r * 28 + c1] for _ in ids])],
                            local_sem=T.sem["snd2a" if b == 0 else "snd2b"])
 
-    def pick(q, i, d):
-        lists = T.lst[:, 4 * (d - 1):4 * d] if i == r else T.ln[:, i * 28 + 4 * (d - 1):i * 28 + 4 * d]
-        out = T.yb[:, i * 512 + d:(i + 1) * 512:8]
-        win = T.kv_s[:, i * 2048:(i + 1) * 2048].indirect(lists)
-        if q == 0:
-            inc(V.tensor_copy(out, win), yv[i])
-        else:
-            inc(S.activation(out, win, AF.Copy), ys[i])
-
-    for d in range(1, 7):
-        wait(S, e_l[d])
-        pick(1, r, d)
-    wait(V, e_zero)
-    pick(0, r, 7)
+    wait(V, l_kv, i_kz)
+    wait(S, e_l[7])
+    for x in range(4, 8):
+        pick(x % 2, r, x)
     wait(Y, yv[r], ys[r], e_root)
     stores = [one(Y.dma_start(T.y[:, r * 512:(r + 1) * 512], T.yb[:, r * 512:(r + 1) * 512]), 16)]
     cut = LISTS[0][0]

from concourse.bass import DstId, RemoteDMATransfer
from concourse.mybir import AluOpType, ActivationFunctionType

OP = AluOpType
AF = ActivationFunctionType
NONE = 2112
REAL = NONE + 1
WIN = REAL + 1984
KW = 2128
EARLY = 512
BATCHES = (4, 22, 64, 128)
S_PART = ((4, 22), (42, 64), (96, 128))
LISTS = ((4, 0, 16), (7, 16, 28))
BIG = 131072.0
LIFT = 4096.0

SCRATCH = {
    "bd": ("dram", [3, 128, 128], "int32"),
    "own": ("sbuf", [128, 128], "int32"),
    "land": ("sbuf", [128, 384], "int32"),
    "mx": ("sbuf", [128, 128], "int32"),
    "tgt": ("sbuf", [128, 128], "int32"),
    "tgtf": ("sbuf", [128, 128], "float32"),
    "parw": ("sbuf", [128, 128], "int32"),
    "tokd": ("sbuf", [128, 128], "int32"),
    "plo32": ("sbuf", [128, 128], "int32"),
    "phi32": ("sbuf", [128, 128], "int32"),
    "plo": ("sbuf", [128, 128], "uint16"),
    "phi": ("sbuf", [128, 128], "bfloat16"),
    "tk": ("sbuf", [128, 128], "float16"),
    "pb": ("sbuf", [128, 16], "int32"),
    "bits": ("sbuf", [128, 24], "int32"),
    "gi": ("sbuf", [128, 1], "int32"),
    "mask": ("sbuf", [128, 24], "float32"),
    "gcol": ("sbuf", [128, 1], "float32"),
    "ccol": ("sbuf", [128, 1], "float32"),
    "lcol": ("sbuf", [128, 1], "float32"),
    "u": ("sbuf", [128, 128], "bfloat16"),
    "gx": ("sbuf", [128, 128], "bfloat16"),
    "k16": ("sbuf", [128, 128], "bfloat16"),
    "wx": ("sbuf", [128, 144], "bfloat16"),
    "x32": ("sbuf", [128, 128], "bfloat16"),
    "ones": ("sbuf", [128, 512], "bfloat16"),
    "bl": ("sbuf", [128, 128], "bfloat16"),
    "gt": ("sbuf", [128, 512], "float16"),
    "gp": ("sbuf", [128, 512], "bfloat16"),
    "tm": ("sbuf", [128, 512], "float16"),
    "hm": ("sbuf", [128, 512], "bfloat16"),
    "wsel": ("sbuf", [128, 144], "bfloat16"),
    "cc0": ("sbuf", [128, 128], "bfloat16"),
    "cc": ("sbuf", [128, 128], "bfloat16"),
    "key": ("sbuf", [128, 2048], "float32"),
    "tg": ("sbuf", [128, 1984], "float32"),
    "eq": ("sbuf", [128, 1984], "bfloat16"),
    "o2": ("sbuf", [128, 128], "float32"),
    "off": ("sbuf", [128, 128], "uint16"),
    "jv": ("sbuf", [128, 1984], "float32"),
    "nv": ("sbuf", [128, WIN], "float32"),
    "ns": ("sbuf", [128, WIN], "float32"),
    "m": ("sbuf", [128, 128], "float32"),
    "sc": ("sbuf", [128, 128], "float32"),
    "lst": ("sbuf", [128, 28], "uint16"),
    "ln": ("sbuf", [128, 112], "uint16"),
    "kv_s": ("sbuf", [128, 4 * KW], "bfloat16"),
    "yb": ("sbuf", [128, 2048], "bfloat16"),
    "psa": ("psum", [128, 2048], "float32"),
    "psb": ("psum", [128, 2048], "float32"),
}
SEMAPHORES = (["snd1a", "snd1b", "snd2a", "snd2b"] + ["arr%d" % o for o in (1, 2, 3)]
              + ["gl%d%d" % (b, i) for b in (0, 1) for i in (0, 1, 2, 3)] + ["e%d" % i for i in range(130)])


def rank_program(g, core, T, topo):
    r = T.rank_of(core)
    if r is None:
        return
    V, S, P, Y = g.vector, g.scalar, g.tensor, g.sync
    N = len(T.cores)
    count, waited = {}, set()

    def ev():
        name = "e%d" % len(count)
        count[name] = 0
        return name

    def inc(ins, name, n=1):
        ins.then_inc(T.sem[name], n)
        count[name] = count[name] + n
        return name

    def wait(q, *names):
        for name in names:
            q.wait_ge(T.sem[name], count[name])
            waited.add(name)

    def one(ins, n=1):
        return inc(ins, ev(), n)

    dst = {o: T.cores[(r + o) % N] for o in (1, 2, 3)}
    order = (1, 3, 2)

    lb = {}

    def part(q):
        return T.best[:, q * 2048:(q + 1) * 2048]

    lb[1] = one(Y.dma_start(T.bd[0], part((r + 1) % N)), 16)
    l_par = one(S.dma_start(T.parw[:], T.par[:]), 16)
    lb[3] = one(Y.dma_start(T.bd[2], part((r + 3) % N)), 16)
    l_tok = one(S.dma_start(T.tokd[:], T.tok[:]), 16)
    lb[2] = one(S.dma_start(T.bd[1], part((r + 2) % N)), 16)
    l_own = one(Y.dma_start(T.own[:], part(r)), 16)
    l_kv = ev()
    inc(Y.dma_start(T.kv_s[:, 0:EARLY], T.kv[:, 0:EARLY]), l_kv, 16)

    flag = dict(allow_small_or_imprecise_dtypes=True)
    i_pb = one(g.iota(T.pb[:], [[-1, 16]], 0, 1))
    i_gx = one(g.iota(T.gx[:], [[16, 8], [0, 16]], 0, 0, **flag))
    i_u = one(g.iota(T.u[:], [[0, 8], [1, 16]], 1, 0, **flag))
    for o in order:
        d = dst[o]
        rid, pid, _ = topo.addr(d)
        wait(g, lb[o])
        g.remote_dma(T.land[:, (o - 1) * 128:o * 128], T.bd[o - 1], T.sem["arr%d" % o],
                     T.sem["snd1b" if o == order[-1] else "snd1a"], pid, rid, topo.mask(core, d))
    n_snd1 = [len(topo.engines(core, dst[o])) for o in order]
    i_k = one(g.iota(T.k16[:], [[16, 128]], 2048, 0, **flag))
    i_w = one(g.iota(T.wx[:], [[1, 144]], -15, 0, **flag))
    i_x = one(g.iota(T.x32[:], [[0, 4], [1, 32]], 0, 0, **flag))
    cut0 = (S_PART[1][0] - 4) * 16
    i_j0 = one(g.iota(T.jv[:, 0:cut0], [[-1, cut0]], NONE - 64, 0, **flag))
    i_j1 = one(g.iota(T.jv[:, cut0:1984], [[-1, 1984 - cut0]], NONE - 64 - cut0, 0, **flag))
    i_kz = ev()
    for i in range(N):
        inc(g.iota(T.kv_s[:, i * KW + 2048:(i + 1) * KW], [[0, KW - 2048]], 0, 0, **flag), i_kz)

    Y.wait_ge(T.sem.snd1a, sum(n_snd1[:-1]))
    inc(Y.dma_start(T.kv_s[:, EARLY:2048], T.kv[:, EARLY:2048]), l_kv, 16)
    for i in range(1, N):
        inc(Y.dma_start(T.kv_s[:, i * KW:i * KW + 2048], T.kv[:, i * 2048:(i + 1) * 2048]), l_kv, 16)

    e_z0 = one(V.memset(T.ns[:, 0:160], 0.0))
    e_one = one(V.memset(T.ones[:], 1.0 / 128))
    wait(V, i_pb)
    a = ev()
    inc(V.tensor_scalar(T.bits[:, 0:16], T.pb[:], 15, None, OP.bitwise_and), a)
    inc(V.tensor_scalar(T.bits[:, 16:20], T.pb[:, 0:4], 3, None, OP.bitwise_and), a)
    inc(V.tensor_scalar(T.bits[:, 20:24], T.pb[:, 0:16:4], 12, None, OP.bitwise_and), a)
    inc(V.tensor_scalar(T.gi[:], T.pb[:, 0:1], 112, None, OP.bitwise_and), a)
    wait(V, a)
    e_col = ev()
    inc(V.tensor_scalar(T.mask[:], T.bits[:], 0.0, None, OP.is_equal), e_col)
    inc(V.tensor_copy(T.gcol[:], T.gi[:]), e_col)
    wait(V, i_gx, e_col)
    e_g = ev()
    for q in range(4):
        inc(V.tensor_scalar(T.gp[:, q * 128:(q + 1) * 128], T.gx[:], T.gcol[:], T.mask[:, 16 + q:17 + q], OP.is_equal, OP.mult), e_g)
    wait(V, i_u)
    e_bl = one(V.tensor_scalar(T.bl[:], T.u[:], -4096.0, 4096.0 + 2048.0, OP.mult, OP.add))

    wait(V, l_par)
    e_hi = one(V.tensor_scalar(T.phi32[:], T.parw[:], 1920, None, OP.bitwise_and))
    e_lo = one(V.tensor_scalar(T.plo32[:], T.parw[:], 127, None, OP.bitwise_and))
    wait(V, e_hi)
    e_phi = one(V.tensor_scalar(T.phi[:], T.phi32[:], 32.0, None, OP.mult))
    e_gt = ev()
    for q in range(4):
        inc(V.tensor_scalar(T.gt[:, q * 128:(q + 1) * 128], T.gx[:], T.gcol[:], T.mask[:, 20 + q:21 + q], OP.is_equal, OP.mult), e_gt)
    wait(V, e_phi)
    e_hm = ev()
    for s in range(4):
        inc(V.tensor_scalar(T.hm[:, s:512:4], T.phi[:], T.mask[:, 20 + s:21 + s], None, OP.mult), e_hm)
    wait(V, l_tok)
    e_tk = one(V.tensor_scalar(T.tk[:], T.tokd[:], -2048.0, None, OP.add))
    wait(V, e_lo)
    e_plo = one(V.tensor_copy(T.plo[:], T.plo32[:]))
    wait(V, e_tk)
    e_tm = ev()
    for q in range(4):
        inc(V.tensor_scalar(T.tm[:, q * 128:(q + 1) * 128], T.tk[:], T.mask[:, 16 + q:17 + q], None, OP.mult), e_tm)
    e_cl = ev()
    inc(V.tensor_scalar(T.ccol[:], T.bits[:, 0:1], -2.0 * BIG, -BIG, OP.mult, OP.add), e_cl)
    inc(V.tensor_scalar(T.lcol[:], T.bits[:, 0:1], -2.0 * LIFT, 30.0 * LIFT + NONE + 0.25, OP.mult, OP.add), e_cl)
    e_fill = one(V.memset(T.nv[:, 0:REAL], 0.0))
    wait(V, i_w)
    e_wsel = one(V.tensor_scalar(T.wsel[:], T.wx[:], T.gcol[:], -8192.0, OP.is_equal, OP.mult))

    wait(S, e_z0)
    e_s = one(S.activation(T.ns[:, 160:320], T.ns[:, 0:160], AF.Silu))
    wait(S, e_s)
    e_s = one(S.activation(T.ns[:, 320:640], T.ns[:, 0:320], AF.Copy))
    wait(S, e_s)
    e_s = one(S.activation(T.ns[:, 640:1280], T.ns[:, 0:640], AF.Copy))
    wait(S, e_s)
    e_s2 = one(S.activation(T.ns[:, 1280:REAL], T.ns[:, 0:REAL - 1280], AF.Copy))

    wait(P, e_one, e_bl)
    for q in range(4):
        P.matmul(T.psb[:, q * 512:(q + 1) * 512], T.bl[:], T.ones[:], True, False)
    wait(P, e_g, e_hm)
    pe_k = []
    for q in range(4):
        for s in range(4):
            P.matmul(T.psb[:, q * 512 + s:(q + 1) * 512:4], T.gp[:, s * 128:(s + 1) * 128], T.hm[:, q * 128:(q + 1) * 128], False, False)
        if q == 0:
            wait(P, e_gt, e_tm)
        pe_k.append(one(P.matmul(T.psb[:, q * 512:(q + 1) * 512], T.gt[:, q * 128:(q + 1) * 128], T.tm[:], False, True)))
    wait(P, i_k, i_u)
    for x in range(len(BATCHES) - 1):
        a, b = BATCHES[x], BATCHES[x + 1]
        out = T.psa[:, 512 * x:512 * x + b - a]
        P.matmul(out, T.ones[:, 0:128], T.k16[:, a:b], True, False)
        P.matmul(out, T.u[:], T.ones[:, 0:b - a], False, False)
    a3 = BATCHES[-2]
    e_key = []
    for q in range(4):
        wait(S, pe_k[q])
        hi = min((q + 1) * 512, a3 * 16)
        if hi > q * 512:
            e_key.append(one(S.activation(T.key[:, q * 512:hi], T.psb[:, q * 512:hi], AF.Copy)))
        else:
            e_key.append(pe_k[q])
    wait(S, i_x, e_cl)
    e_c0 = one(S.activation(T.cc0[:], T.x32[:], AF.Identity, bias=T.ccol[:], scale=BIG))

    wait(V, l_own)
    run = T.psa[:, 1536:1664]
    src = T.own[:]
    for n, o in enumerate(order):
        sender = T.cores[(r - o) % N]
        V.wait_ge(T.sem["arr%d" % o], len(topo.engines(sender, core)))
        out = run if n < 2 else T.mx[:]
        e = one(V.tensor_tensor(out, src, T.land[:, (o - 1) * 128:o * 128], OP.max))
        wait(V, e)
        src = out
    e_tgt = one(V.tensor_scalar(T.tgt[:], T.mx[:], 4095, None, OP.bitwise_and))
    wait(V, e_tgt, e_plo)

    def match(x):
        a, b = BATCHES[x], BATCHES[x + 1]
        wait(V, *[e_key[q] for q in range(4) if q * 32 < b and a < (q + 1) * 32])
        return one(V.tensor_tensor(T.eq[:, (a - 4) * 16:(b - 4) * 16], T.tgt[:, 0:128].indirect(T.plo[:, a:b]),
                                   T.key[:, a * 16:b * 16], OP.is_equal))

    def gather_bits(x, e_m):
        a, b = BATCHES[x], BATCHES[x + 1]
        wait(P, e_m)
        for i in range(16):
            ins = P.matmul(T.psa[:, 512 * x:512 * x + b - a], T.wsel[:, 15 - i:143 - i],
                           T.eq[:, (a - 4) * 16 + i:(b - 4) * 16:16], False, i == 15)
        return one(ins)

    def offsets(x, e_ok):
        a, b = BATCHES[x], BATCHES[x + 1]
        wait(V, e_ok)
        e = one(V.tensor_tensor(T.o2[:, a:b], T.psa[:, 512 * x:512 * x + b - a], T.parw[:, a:b], OP.max))
        wait(V, e)
        return one(V.tensor_copy(T.off[:, a:b], T.o2[:, a:b]))

    def scatter_v(a, b):
        return one(V.tensor_copy(T.nv[:, 0:WIN].indirect(T.off[:, a:b]), T.jv[:, (a - 4) * 16:(b - 4) * 16]))

    def scatter_s(a, b):
        return one(S.activation(T.ns[:, 0:WIN].indirect(T.off[:, a:b]), T.jv[:, (a - 4) * 16:(b - 4) * 16], AF.Silu))

    wait(P, e_wsel)
    last = {"s": None, "v": None}

    def scatters(x, e_off):
        a, b = BATCHES[x], BATCHES[x + 1]
        sa, sb = S_PART[x]
        wait(S, e_off)
        if last["s"]:
            wait(S, last["s"])
        else:
            wait(S, e_s2, i_j0)
        if x == 1:
            wait(S, i_j1)
        last["s"] = scatter_s(sa, sb)
        if a < sa:
            wait(V, e_off)
            if last["v"]:
                wait(V, last["v"])
            else:
                wait(V, e_fill, i_j0)
            if x == 2:
                wait(V, i_j1)
            last["v"] = scatter_v(a, sa)

    e_tf = one(V.tensor_copy(T.tgtf[:], T.tgt[:]))
    wait(S, e_tf, e_plo)
    c3, d3 = (a3 - 4) * 16, 1984
    e_tg = one(S.activation(T.tg[:, c3:d3], T.tgtf[:, 0:128].indirect(T.plo[:, a3:128]), AF.Copy))
    ok0 = gather_bits(0, match(0))
    ok1 = gather_bits(1, match(1))
    wait(V, e_c0)
    e_cc = one(V.tensor_scalar(T.cc[:], T.cc0[:], LIFT, None, OP.min))
    scatters(0, offsets(0, ok0))
    wait(V, e_tg, *[e_key[q] for q in range(4)])
    e = ev()
    mid = c3
    while mid < d3:
        end = min(d3, (mid + 64) // 512 * 512 + 512 - 64)
        inc(V.tensor_tensor(T.eq[:, mid:end], T.tg[:, mid:end], T.psb[:, mid + 64:end + 64], OP.is_equal), e)
        mid = end
    ok2 = gather_bits(2, e)
    scatters(1, offsets(1, ok1))
    scatters(2, offsets(2, ok2))

    ys = [ev() for i in range(N)]
    yv = [ev() for i in range(N)]
    e_root = ev()

    def pick(q, i, d):
        lists = T.lst[:, 4 * (d - 1):4 * d] if i == r else T.ln[:, i * 28 + 4 * (d - 1):i * 28 + 4 * d]
        out = T.yb[:, i * 512 + d:(i + 1) * 512:8]
        win = T.kv_s[:, i * KW:i * KW + REAL].indirect(lists)
        if q == 0:
            inc(V.tensor_copy(out, win), yv[i])
        else:
            inc(S.activation(out, win, AF.Copy), ys[i])

    wait(V, last["v"], e_cc, e_cl)
    wait(S, last["s"])
    e_l = {}
    for d in range(1, 8):
        if d == 1:
            e_a = one(V.tensor_copy(T.m[:, 0:128:2], T.nv[:, 0:64]))
            e_b = one(S.activation(T.m[:, 1:128:2], T.ns[:, 0:64], AF.Copy))
        else:
            lists = T.lst[:, 4 * (d - 2):4 * (d - 1)]
            wait(S, e_l[d - 1])
            e_a = one(V.tensor_copy(T.m[:, 0:128:2], T.nv[:, 0:REAL].indirect(lists)))
            e_b = one(S.activation(T.m[:, 1:128:2], T.ns[:, 0:REAL].indirect(lists), AF.Copy))
        wait(V, e_a, e_b)
        e = one(V.tensor_tensor_scan(T.sc[:], T.cc[:], T.m[:], 0.0, OP.add, OP.max))
        wait(V, e)
        e_l[d] = one(V.tensor_scalar(T.lst[:, 4 * (d - 1):4 * d], T.sc[:, 31:128:32], -1.0, T.lcol[:], OP.mult, OP.add))
        wait(V, e_l[d])
        if d == 4:
            wait(S, l_kv, i_kz)
        if d >= 4:
            for x in (d - 4, d):
                if x < N:
                    inc(S.activation(T.yb[:, x * 512:(x + 1) * 512:8], T.kv_s[:, x * KW:x * KW + 64], AF.Copy), e_root)
                elif x >= 5:
                    pick(1, r, x - 4)

    mask = topo.mask(core, dst[1]) & topo.mask(core, dst[2]) & topo.mask(core, dst[3])
    bits = bin(mask).count("1")
    ids = [DstId(rid=topo.addr(dst[o])[0], pnc=topo.addr(dst[o])[1]) for o in order]
    for b, (d, c0, c1) in enumerate(LISTS):
        wait(g, e_l[d])
        g.remote_dma_fused([RemoteDMATransfer(dst_ids=ids, dma_engine_mask=mask, remote_sem=T.sem["gl%d%d" % (b, r)],
                                              srcs=[T.lst[:, c0:c1]], dsts=[T.ln[:, r * 28 + c0:r * 28 + c1] for _ in ids])],
                           local_sem=T.sem["snd2a" if b == 0 else "snd2b"])

    wait(V, l_kv, i_kz)
    wait(S, e_l[7])
    for x in range(4, 8):
        pick(x % 2, r, x)
    wait(Y, yv[r], ys[r], e_root)
    stores = [one(Y.dma_start(T.y[:, r * 512:(r + 1) * 512], T.yb[:, r * 512:(r + 1) * 512]), 16)]
    cut = LISTS[0][0]
    for b, ds in enumerate((range(1, cut + 1), range(cut + 1, 8))):
        n = 0
        for o in order:
            i = (r - o) % N
            V.wait_ge(T.sem["gl%d%d" % (b, i)], bits)
            S.wait_ge(T.sem["gl%d%d" % (b, i)], bits)
            for d in ds:
                pick(n % 2, i, d)
                n = n + 1
    for o in order:
        i = (r - o) % N
        wait(Y, yv[i], ys[i])
        stores.append(one(Y.dma_start(T.y[:, i * 512:(i + 1) * 512], T.yb[:, i * 512:(i + 1) * 512]), 16))
    for e in stores:
        wait(Y, e)
    g.wait_ge(T.sem.snd1b, n_snd1[-1])
    g.wait_ge(T.sem.snd2a, bits)
    g.wait_ge(T.sem.snd2b, bits)
    for e in list(count):
        if e not in waited and count[e]:
            wait(g, e)
